import numpy as np
import ml_dtypes


def mxq(x, axis, fmt="e4m3"):
    dtype, down = {"e4m3": (ml_dtypes.float8_e4m3fn, 7), "e5m2": (ml_dtypes.float8_e5m2, 14)}[fmt]
    v = np.moveaxis(np.asarray(x, np.float32).astype(ml_dtypes.bfloat16).astype(np.float64), axis, -1)
    blocks = v.reshape(v.shape[:-1] + (-1, 32))
    amax = np.abs(blocks).max(-1, keepdims=True)
    byte = np.maximum(np.where(amax > 0, np.frexp(amax)[1] - 1 + 127, 0) - down, 1)
    scale = np.exp2(byte - 127.0)
    codes = (blocks / scale).astype(np.float32).astype(dtype).astype(np.float64)
    return np.moveaxis((codes * scale).reshape(v.shape), -1, axis)


WIDE = False


def mx_kscale(k):
    if not WIDE:
        return np.ones(k)
    levels = np.array([30, -30])
    if k % 512:
        return np.exp2(np.random.permutation(np.resize(levels, k // 32))).repeat(32)
    a = np.empty((k // 512, 16))
    for p in range(k // 512):
        a[p, :8] = np.random.permutation(np.resize(levels, 8))
        for g in range(8):
            far = levels[np.abs(levels - a[p, g]) >= 10]
            a[p, g + 8] = far[np.random.randint(len(far))]
    return np.exp2(a.ravel()).repeat(32)


BF16 = ml_dtypes.bfloat16


def bf(x):
    return np.asarray(x, np.float32).astype(BF16)


def f64(x):
    return np.asarray(x).astype(np.float64)

E4M3FN = np.array([(-1.0 if i & 128 else 1.0) * ((1.0 + (i & 7) / 8.0) * 2.0 ** (((i >> 3) & 15) - 7) if i & 120 else (i & 7) * 2.0 ** -9) for i in range(256)])


def e4m3fn_bytes(y):
    return np.clip(np.asarray(y, np.float64), -448.0, 448.0).astype(np.float32).astype(ml_dtypes.float8_e4m3fn).view(np.uint8)


def e4m3fn_values(b):
    return E4M3FN[b]

def planes(Y):
    n, m = Y.shape
    b = f64(bf(Y)).reshape(n // 32, 32, m)
    amax = np.abs(b).max(1)
    byte = np.clip(np.where(amax > 0, np.frexp(amax)[1] - 1 + 127 - 7, 1), 1, 254)
    codes = (b * np.exp2(127.0 - byte)[:, None, :]).reshape(n, m).astype(np.float32).astype(ml_dtypes.float8_e4m3fn).view(np.uint8)
    words = codes.reshape(n // 512, 128, 4, m).transpose(0, 1, 3, 2)
    return np.ascontiguousarray(words), np.ascontiguousarray(byte.astype(np.uint8).reshape(n // 512, 16, m))


T, K, N, KB = 1024, 2048, 1024, 32

FP8_MAX = 448.0
TAIL = 4.0


def setup_inputs():
    s = mx_kscale(K)
    vol = np.exp(0.5 * np.random.randn(T, 1))
    R = vol * np.random.standard_t(TAIL, (T, K)) * s[None, :]
    R_scale = (np.abs(R).reshape(T, K // KB, KB).max(axis=2) / FP8_MAX).astype(np.float32)
    R_bytes = e4m3fn_bytes(R / np.repeat(f64(R_scale), KB, axis=1))
    B = np.random.randn(K, N) / np.sqrt(K) / s[:, None]
    gain = np.exp(0.8 * np.random.randn(1, N))
    return {
        "R_bytes": R_bytes,
        "R_scale": R_scale,
        "B": bf(B),
        "inv_vol": bf(1.0 / vol),
        "gain": bf(gain),
    }


def reference(R_bytes, R_scale, B, inv_vol, gain):
    R = e4m3fn_values(R_bytes) * np.repeat(f64(R_scale), KB, axis=1)
    z = mxq(R, 1, "e5m2") @ mxq(f64(B), 0, "e4m3")
    u = z * f64(inv_vol)
    y = np.sign(u) * np.log1p(np.abs(u)) * f64(gain)
    words, scales = planes(y.T)
    return y, words, scales

@@ -1,0 +1,285 @@
+from contextlib import ExitStack
+
+import concourse.mybir as mybir
+from concourse.masks import make_identity
+
+T, K, N, KB = 1024, 2048, 1024, 32
+FLOPS = 2 * T * K * N
+
+F32 = mybir.dt.float32
+BF16 = mybir.dt.bfloat16
+U32 = mybir.dt.uint32
+I32 = mybir.dt.int32
+U8 = mybir.dt.uint8
+FP8 = mybir.dt.float8_e4m3fn
+E4X4 = mybir.dt.float8_e4m3fn_x4
+E5X4 = mybir.dt.float8_e5m2_x4
+ACT = mybir.ActivationFunctionType
+ALU = mybir.AluOpType
+
+P = 128
+PACK = 4
+K_PASS = P * PACK
+PASSES = K // K_PASS
+DAY_TILES = T // P
+N_TILE = 512
+HALVES = N // N_TILE
+CHUNK = 2 * K_PASS
+CHUNKS = DAY_TILES * K // CHUNK
+BLOCKS = CHUNK // KB
+UNITS = DAY_TILES * HALVES
+EARLY_TILES = 2
+
+
+def tile_factor_return_symlog_b13_kernel(tc, R_bytes, R_scale, B, inv_vol, gain, out_0, out_1, out_2):
+    nc = tc.nc
+    with ExitStack() as ctx:
+        keep = ctx.enter_context(tc.tile_pool(name="keep", bufs=1))
+        work = ctx.enter_context(tc.tile_pool(name="work", bufs=3))
+        psum = ctx.enter_context(tc.psum_pool(name="psum", bufs=2))
+        ctx.enter_context(tc.manual_schedule())
+
+        ident = keep.tile([P, P], F32, name="ident")
+        iv_rows = keep.tile([P, P], BF16, name="iv_rows")
+        warm = keep.tile([P, 1], F32, name="warm")
+        warm_out = keep.tile([P, 1], F32, name="warm_out")
+        nc.vector.memset(warm[:], 1.0)
+        nc.scalar.activation(out=warm_out[:], in_=warm[:], func=ACT.Ln)
+        nc.gpsimd.memset(iv_rows[:], 0.0)
+        make_identity(nc, ident[:])
+
+        scale_view = R_scale.rearrange("(t p) b -> p t b", p=P)
+        rs_early = keep.tile([P, EARLY_TILES, K // KB], F32, name="rs_early")
+        rs_late = keep.tile([P, DAY_TILES - EARLY_TILES, K // KB], F32, name="rs_late")
+        r_raw = [keep.tile([P, K], U8, name="r_raw%d" % t) for t in range(DAY_TILES)]
+        b_raw = {}
+        for h in range(HALVES):
+            for g in range(PASSES):
+                b_raw[(g, h)] = keep.tile([P, PACK, N_TILE], BF16, name="b_raw%d_%d" % (g, h))
+        gain_bc = keep.tile([P, N], BF16, name="gain_bc")
+
+        def load_r(t):
+            nc.sync.dma_start(out=r_raw[t][:], in_=R_bytes[t * P : (t + 1) * P, :])
+
+        def load_b(g, h):
+            rows = B[g * K_PASS : (g + 1) * K_PASS, h * N_TILE : (h + 1) * N_TILE]
+            nc.sync.dma_start(out=b_raw[(g, h)][:], in_=rows.rearrange("(p j) n -> p j n", j=PACK))
+
+        nc.sync.dma_start(out=rs_early[:], in_=scale_view[:, :EARLY_TILES, :])
+        load_r(0)
+        load_b(0, 0)
+        load_b(1, 0)
+        load_r(1)
+        load_b(2, 0)
+        nc.sync.dma_start(out=rs_late[:], in_=scale_view[:, EARLY_TILES:, :])
+        load_b(3, 0)
+        load_r(2)
+        nc.sync.dma_start(out=iv_rows[:DAY_TILES, :], in_=inv_vol.rearrange("(t p) o -> t (p o)", p=P))
+        nc.sync.dma_start(out=gain_bc[:], in_=gain.rearrange("o n -> (o n)").partition_broadcast(P))
+        for g in range(PASSES):
+            load_r(3 + g)
+            load_b(g, 1)
+        load_r(7)
+
+        r_wide, r_bank, r_grouped, r_codes, r_scales = {}, {}, {}, {}, {}
+        b_grouped, b_codes, b_scales = {}, {}, {}
+        z, mag, sgn, lg, sg, y, y_half, y_bank, y_grouped = {}, {}, {}, {}, {}, {}, {}, {}, {}
+        iv = keep.tile([P, DAY_TILES], F32, name="iv")
+        y_scales = keep.tile([P, HALVES, T], U8, name="y_scales", align_bytes=64)
+
+        def scale_cols(c):
+            t, half = divmod(c, 2)
+            tile = rs_early[:, t, :] if t < EARLY_TILES else rs_late[:, t - EARLY_TILES, :]
+            return tile[:, half * BLOCKS : (half + 1) * BLOCKS]
+
+        def widen(c):
+            t, half = divmod(c, 2)
+            src = r_raw[t][:, half * CHUNK : (half + 1) * CHUNK].bitcast(FP8)
+            r_wide[c] = work.tile([P, CHUNK], BF16, name="r_wide", bufs=6)
+            cols = scale_cols(c)
+            for b in range(BLOCKS):
+                span = slice(b * KB, (b + 1) * KB)
+                nc.scalar.activation(out=r_wide[c][:, span], in_=src[:, span], func=ACT.Copy, scale=cols[:, b : b + 1])
+
+        def widen_v(c):
+            t, half = divmod(c, 2)
+            src = r_raw[t][:, half * CHUNK : (half + 1) * CHUNK].bitcast(FP8)
+            r_wide[c] = work.tile([P, CHUNK], BF16, name="r_wide", bufs=6)
+            cols = scale_cols(c)
+            for b in range(BLOCKS):
+                span = slice(b * KB, (b + 1) * KB)
+                nc.vector.tensor_scalar(out=r_wide[c][:, span], in0=src[:, span], scalar1=cols[:, b : b + 1], scalar2=None, op0=ALU.mult)
+
+        def turn_r(c):
+            words = r_wide[c][:].bitcast(F32)
+            r_bank[c] = psum.tile([P, 4, P], F32, name="r_bank", bufs=2)
+            for gl in range(2):
+                for u in range(2):
+                    nc.tensor.transpose(r_bank[c][:, 2 * gl + u, :], words[:, 256 * gl + u : 256 * (gl + 1) : 2], ident[:])
+
+        def exit_r(c):
+            r_grouped[c] = work.tile([P, CHUNK], BF16, name="r_grouped", align_bytes=64)
+            nc.vector.tensor_copy(
+                out=r_grouped[c][:].bitcast(F32).rearrange("p (g r u) -> p g r u", g=2, u=2),
+                in_=r_bank[c][:].rearrange("p (g u) r -> p g r u", u=2),
+            )
+
+        def quant_r(c):
+            r_codes[c] = keep.tile([P, 2 * P], U32, name="r_codes%d" % c, align_bytes=64)
+            r_scales[c] = keep.tile([P, 2 * P], U8, name="r_scales%d" % c, align_bytes=64)
+            nc.vector.quantize_mx(out=r_codes[c][:].bitcast(E5X4), scales=r_scales[c][:], in_=r_grouped[c][:])
+
+        def weave_b(g, h):
+            b_grouped[(g, h)] = work.tile([P, N_TILE, PACK], BF16, name="b_grouped", align_bytes=64)
+            nc.vector.tensor_copy(
+                out=b_grouped[(g, h)][:].rearrange("p (c i) t -> p c t i", i=4),
+                in_=b_raw[(g, h)][:].rearrange("p t (c i) -> p c t i", i=4),
+            )
+
+        def quant_b(g, h):
+            b_codes[(g, h)] = keep.tile([P, N_TILE], U32, name="b_codes%d_%d" % (g, h), align_bytes=64)
+            b_scales[(g, h)] = keep.tile([P, N_TILE], U8, name="b_scales%d_%d" % (g, h), align_bytes=64)
+            nc.vector.quantize_mx(
+                out=b_codes[(g, h)][:].bitcast(E4X4),
+                scales=b_scales[(g, h)][:],
+                in_=b_grouped[(g, h)][:].rearrange("p n t -> p (n t)"),
+            )
+
+        def multiply(i):
+            h, t = divmod(i, DAY_TILES)
+            z[i] = psum.tile([P, N_TILE], F32, name="z", bufs=4)
+            for g in range(PASSES):
+                c, gl = 2 * t + g // 2, g % 2
+                cols = slice(gl * P, (gl + 1) * P)
+                nc.tensor.matmul_mx(
+                    out=z[i][:],
+                    lhsT=r_codes[c][:, cols].bitcast(E5X4),
+                    lhsT_scale=r_scales[c][:, cols],
+                    rhs=b_codes[(g, h)][:].bitcast(E4X4),
+                    rhs_scale=b_scales[(g, h)][:],
+                    start=(g == 0),
+                    stop=(g == PASSES - 1),
+                )
+
+        def compress(i):
+            t = i % DAY_TILES
+            mag[i] = work.tile([P, N_TILE], F32, name="mag", bufs=2)
+            sgn[i] = work.tile([P, N_TILE], BF16, name="sgn")
+            lg[i] = work.tile([P, N_TILE], F32, name="lg")
+            nc.scalar.activation(out=mag[i][:], in_=z[i][:], func=ACT.Abs, scale=iv[:, t : t + 1])
+            nc.scalar.activation(out=sgn[i][:], in_=z[i][:], func=ACT.Sign, scale=iv[:, t : t + 1])
+            nc.scalar.activation(out=lg[i][:], in_=mag[i][:], func=ACT.Ln, bias=1.0)
+
+        def signed_gain(i):
+            h = i // DAY_TILES
+            sg[i] = work.tile([P, N_TILE], BF16, name="sg", bufs=2)
+            nc.vector.tensor_tensor(out=sg[i][:], in0=sgn[i][:], in1=gain_bc[:, h * N_TILE : (h + 1) * N_TILE], op=ALU.mult)
+
+        def finish(i):
+            h, t = divmod(i, DAY_TILES)
+            y[i] = work.tile([P, N_TILE], F32, name="y", bufs=4)
+            nc.vector.tensor_tensor(out=y[i][:], in0=lg[i][:], in1=sg[i][:], op=ALU.mult)
+            nc.sync.dma_start(out=out_0[t * P : (t + 1) * P, h * N_TILE : (h + 1) * N_TILE], in_=y[i][:])
+
+        def round_y(i):
+            y_half[i] = work.tile([P, N_TILE], BF16, name="y_half")
+            nc.vector.tensor_copy(out=y_half[i][:], in_=y[i][:])
+            words = y_half[i][:].bitcast(F32)
+            y_bank[i] = psum.tile([P, 2, P], F32, name="y_bank", bufs=2)
+            for u in range(2):
+                nc.tensor.transpose(y_bank[i][:, u, :], words[:, u : 256 : 2], ident[:])
+
+        def exit_y(i):
+            y_grouped[i] = work.tile([P, N_TILE], BF16, name="y_grouped", align_bytes=64)
+            nc.vector.tensor_copy(
+                out=y_grouped[i][:].bitcast(F32).rearrange("p (r u) -> p r u", u=2),
+                in_=y_bank[i][:].rearrange("p u r -> p r u"),
+            )
+
+        def quant_y(i):
+            h, t = divmod(i, DAY_TILES)
+            days = slice(t * P, (t + 1) * P)
+            codes = work.tile([P, P], U32, name="y_codes", bufs=4, align_bytes=64)
+            nc.vector.quantize_mx(out=codes[:].bitcast(E4X4), scales=y_scales[:, h, days], in_=y_grouped[i][:])
+            words_out = out_1[h].rearrange("p m t -> p (m t)").bitcast(I32)
+            nc.sync.dma_start(out=words_out[:, days], in_=codes[:].bitcast(I32))
+            if t == DAY_TILES - 1:
+                for q in range(4):
+                    queue = nc.sync if q % 2 == 0 or h == 0 else nc.scalar
+                    queue.dma_start(
+                        out=out_2[h, 4 * q : 4 * q + 4, :].bitcast(I32),
+                        in_=y_scales[32 * q : 32 * q + 4, h, :].bitcast(I32),
+                    )
+
+        widen_v(1)
+        widen(0)
+        weave_b(0, 0)
+        turn_r(0)
+        turn_r(1)
+        widen(2)
+        weave_b(1, 0)
+        quant_b(0, 0)
+        exit_r(0)
+        weave_b(2, 0)
+        quant_b(1, 0)
+        quant_r(0)
+        exit_r(1)
+        widen(3)
+        turn_r(2)
+        iv_wide = keep.tile([P, P], F32, name="iv_wide")
+        weave_b(3, 0)
+        quant_b(2, 0)
+        quant_r(1)
+        nc.vector.tensor_copy(out=iv_wide[:], in_=iv_rows[:])
+        iv_bank = psum.tile([P, 2, P], F32, name="y_bank", bufs=2)
+        nc.tensor.transpose(iv_bank[:, 0, :], iv_wide[:], ident[:])
+        turn_r(3)
+        quant_b(3, 0)
+        multiply(0)
+        nc.vector.tensor_copy(out=iv[:], in_=iv_bank[:, 0, :DAY_TILES])
+        exit_r(2)
+        exit_r(3)
+        quant_r(2)
+        quant_r(3)
+        widen(4)
+        widen(5)
+
+        issued = 1
+        for i in range(UNITS):
+            c0, c1 = 2 * i + 4, 2 * i + 5
+            chunks = c0 < CHUNKS
+            if chunks:
+                turn_r(c0)
+                turn_r(c1)
+            ahead = min(i + 1 if chunks else i + 2, UNITS - 1)
+            while issued <= ahead:
+                multiply(issued)
+                issued = issued + 1
+            compress(i)
+            if i < PASSES:
+                weave_b(i, 1)
+            if chunks:
+                exit_r(c0)
+            if i < PASSES:
+                quant_b(i, 1)
+            signed_gain(i)
+            if i >= 1:
+                round_y(i - 1)
+            if chunks:
+                exit_r(c1)
+                quant_r(c0)
+            if i >= 2:
+                exit_y(i - 2)
+            finish(i)
+            if chunks:
+                quant_r(c1)
+            if i >= 2:
+                quant_y(i - 2)
+            if c1 + 2 < CHUNKS:
+                widen(c0 + 2)
+                widen(c1 + 2)
+        exit_y(UNITS - 2)
+        round_y(UNITS - 1)
+        quant_y(UNITS - 2)
+        exit_y(UNITS - 1)
+        quant_y(UNITS - 1)

@@ -29,6 +29,9 @@ CHUNKS = DAY_TILES * K // CHUNK
 BLOCKS = CHUNK // KB
 UNITS = DAY_TILES * HALVES
 EARLY_TILES = 2
+EXIT_LAG = 2
+FIRST_MULTIPLY = 10
+AHEAD = 3
 
 
 def tile_factor_return_symlog_b13_kernel(tc, R_bytes, R_scale, B, inv_vol, gain, out_0, out_1, out_2):
@@ -68,18 +71,18 @@ def tile_factor_return_symlog_b13_kernel(tc, R_bytes, R_scale, B, inv_vol, gain,
         nc.sync.dma_start(out=rs_early[:], in_=scale_view[:, :EARLY_TILES, :])
         load_r(0)
         load_b(0, 0)
-        load_b(1, 0)
         load_r(1)
-        load_b(2, 0)
+        load_b(1, 0)
         nc.sync.dma_start(out=rs_late[:], in_=scale_view[:, EARLY_TILES:, :])
-        load_b(3, 0)
         load_r(2)
+        load_b(2, 0)
+        load_r(3)
+        load_b(3, 0)
         nc.sync.dma_start(out=iv_rows[:DAY_TILES, :], in_=inv_vol.rearrange("(t p) o -> t (p o)", p=P))
         nc.sync.dma_start(out=gain_bc[:], in_=gain.rearrange("o n -> (o n)").partition_broadcast(P))
         for g in range(PASSES):
-            load_r(3 + g)
+            load_r(4 + g)
             load_b(g, 1)
-        load_r(7)
 
         r_wide, r_bank, r_grouped, r_codes, r_scales = {}, {}, {}, {}, {}
         b_grouped, b_codes, b_scales = {}, {}, {}
@@ -92,23 +95,17 @@ def tile_factor_return_symlog_b13_kernel(tc, R_bytes, R_scale, B, inv_vol, gain,
             tile = rs_early[:, t, :] if t < EARLY_TILES else rs_late[:, t - EARLY_TILES, :]
             return tile[:, half * BLOCKS : (half + 1) * BLOCKS]
 
-        def widen(c):
+        def widen(c, on_vector):
             t, half = divmod(c, 2)
             src = r_raw[t][:, half * CHUNK : (half + 1) * CHUNK].bitcast(FP8)
             r_wide[c] = work.tile([P, CHUNK], BF16, name="r_wide", bufs=6)
             cols = scale_cols(c)
             for b in range(BLOCKS):
                 span = slice(b * KB, (b + 1) * KB)
-                nc.scalar.activation(out=r_wide[c][:, span], in_=src[:, span], func=ACT.Copy, scale=cols[:, b : b + 1])
-
-        def widen_v(c):
-            t, half = divmod(c, 2)
-            src = r_raw[t][:, half * CHUNK : (half + 1) * CHUNK].bitcast(FP8)
-            r_wide[c] = work.tile([P, CHUNK], BF16, name="r_wide", bufs=6)
-            cols = scale_cols(c)
-            for b in range(BLOCKS):
-                span = slice(b * KB, (b + 1) * KB)
-                nc.vector.tensor_scalar(out=r_wide[c][:, span], in0=src[:, span], scalar1=cols[:, b : b + 1], scalar2=None, op0=ALU.mult)
+                if b < BLOCKS - on_vector:
+                    nc.scalar.activation(out=r_wide[c][:, span], in_=src[:, span], func=ACT.Copy, scale=cols[:, b : b + 1])
+                else:
+                    nc.vector.tensor_scalar(out=r_wide[c][:, span], in0=src[:, span], scalar1=cols[:, b : b + 1], scalar2=None, op0=ALU.mult)
 
         def turn_r(c):
             words = r_wide[c][:].bitcast(F32)
@@ -164,8 +161,8 @@ def tile_factor_return_symlog_b13_kernel(tc, R_bytes, R_scale, B, inv_vol, gain,
         def compress(i):
             t = i % DAY_TILES
             mag[i] = work.tile([P, N_TILE], F32, name="mag", bufs=2)
-            sgn[i] = work.tile([P, N_TILE], BF16, name="sgn")
-            lg[i] = work.tile([P, N_TILE], F32, name="lg")
+            sgn[i] = work.tile([P, N_TILE], BF16, name="sgn", bufs=5)
+            lg[i] = work.tile([P, N_TILE], F32, name="lg", bufs=5)
             nc.scalar.activation(out=mag[i][:], in_=z[i][:], func=ACT.Abs, scale=iv[:, t : t + 1])
             nc.scalar.activation(out=sgn[i][:], in_=z[i][:], func=ACT.Sign, scale=iv[:, t : t + 1])
             nc.scalar.activation(out=lg[i][:], in_=mag[i][:], func=ACT.Ln, bias=1.0)
@@ -181,17 +178,25 @@ def tile_factor_return_symlog_b13_kernel(tc, R_bytes, R_scale, B, inv_vol, gain,
             nc.vector.tensor_tensor(out=y[i][:], in0=lg[i][:], in1=sg[i][:], op=ALU.mult)
             nc.sync.dma_start(out=out_0[t * P : (t + 1) * P, h * N_TILE : (h + 1) * N_TILE], in_=y[i][:])
 
+        def by_half(tile):
+            return tile[:].rearrange("p (q u e) -> p u q e", u=2, e=2)
+
         def round_y(i):
             y_half[i] = work.tile([P, N_TILE], BF16, name="y_half")
-            nc.vector.tensor_copy(out=y_half[i][:], in_=y[i][:])
+            sorted_out = y_half[i][:].rearrange("p (u q e) -> p u q e", u=2, e=2)
+            if i == UNITS - 1:
+                nc.vector.tensor_tensor(out=sorted_out, in0=by_half(lg[i]), in1=by_half(sg[i]), op=ALU.mult)
+            else:
+                nc.vector.tensor_copy(out=sorted_out, in_=by_half(y[i]))
             words = y_half[i][:].bitcast(F32)
             y_bank[i] = psum.tile([P, 2, P], F32, name="y_bank", bufs=2)
             for u in range(2):
-                nc.tensor.transpose(y_bank[i][:, u, :], words[:, u : 256 : 2], ident[:])
+                nc.tensor.transpose(y_bank[i][:, u, :], words[:, u * P : (u + 1) * P], ident[:])
 
         def exit_y(i):
             y_grouped[i] = work.tile([P, N_TILE], BF16, name="y_grouped", align_bytes=64)
-            nc.vector.tensor_copy(
+            copy = nc.scalar.copy if i >= UNITS - 3 else nc.vector.tensor_copy
+            copy(
                 out=y_grouped[i][:].bitcast(F32).rearrange("p (r u) -> p r u", u=2),
                 in_=y_bank[i][:].rearrange("p u r -> p r u"),
             )
@@ -211,75 +216,48 @@ def tile_factor_return_symlog_b13_kernel(tc, R_bytes, R_scale, B, inv_vol, gain,
                         in_=y_scales[32 * q : 32 * q + 4, h, :].bitcast(I32),
                     )
 
-        widen_v(1)
-        widen(0)
-        weave_b(0, 0)
-        turn_r(0)
-        turn_r(1)
-        widen(2)
-        weave_b(1, 0)
-        quant_b(0, 0)
-        exit_r(0)
-        weave_b(2, 0)
-        quant_b(1, 0)
-        quant_r(0)
-        exit_r(1)
-        widen(3)
-        turn_r(2)
+        pieces = [(g, h) for h in range(HALVES) for g in range(PASSES)]
         iv_wide = keep.tile([P, P], F32, name="iv_wide")
-        weave_b(3, 0)
-        quant_b(2, 0)
-        quant_r(1)
-        nc.vector.tensor_copy(out=iv_wide[:], in_=iv_rows[:])
-        iv_bank = psum.tile([P, 2, P], F32, name="y_bank", bufs=2)
-        nc.tensor.transpose(iv_bank[:, 0, :], iv_wide[:], ident[:])
-        turn_r(3)
-        quant_b(3, 0)
-        multiply(0)
-        nc.vector.tensor_copy(out=iv[:], in_=iv_bank[:, 0, :DAY_TILES])
-        exit_r(2)
-        exit_r(3)
-        quant_r(2)
-        quant_r(3)
-        widen(4)
-        widen(5)
-
-        issued = 1
+        issued = 0
+        for c in range(CHUNKS + EXIT_LAG + 1):
+            if c < CHUNKS:
+                widen(c, {1: BLOCKS, CHUNKS - 1: BLOCKS // 2}.get(c, 0))
+            if c % 2 == 1 and c // 2 < len(pieces):
+                weave_b(*pieces[c // 2])
+            if 0 <= c - EXIT_LAG < CHUNKS:
+                turn_r(c - EXIT_LAG)
+            if c == FIRST_MULTIPLY - 1:
+                nc.vector.tensor_copy(out=iv_wide[:], in_=iv_rows[:])
+                iv_bank = psum.tile([P, 2, P], F32, name="y_bank", bufs=2)
+                nc.tensor.transpose(iv_bank[:, 0, :], iv_wide[:], ident[:])
+            if c >= FIRST_MULTIPLY and issued <= AHEAD:
+                multiply(issued)
+                issued = issued + 1
+            if 0 <= c - EXIT_LAG < CHUNKS:
+                exit_r(c - EXIT_LAG)
+            if c == FIRST_MULTIPLY:
+                nc.vector.tensor_copy(out=iv[:], in_=iv_bank[:, 0, :DAY_TILES])
+            if c % 2 == 0 and 0 <= c // 2 - 1 < len(pieces):
+                quant_b(*pieces[c // 2 - 1])
+            if 0 <= c - EXIT_LAG - 1 < CHUNKS:
+                quant_r(c - EXIT_LAG - 1)
+        last = UNITS - 1
         for i in range(UNITS):
-            c0, c1 = 2 * i + 4, 2 * i + 5
-            chunks = c0 < CHUNKS
-            if chunks:
-                turn_r(c0)
-                turn_r(c1)
-            ahead = min(i + 1 if chunks else i + 2, UNITS - 1)
-            while issued <= ahead:
+            if issued <= min(i + AHEAD, last):
                 multiply(issued)
                 issued = issued + 1
             compress(i)
-            if i < PASSES:
-                weave_b(i, 1)
-            if chunks:
-                exit_r(c0)
-            if i < PASSES:
-                quant_b(i, 1)
             signed_gain(i)
             if i >= 1:
                 round_y(i - 1)
-            if chunks:
-                exit_r(c1)
-                quant_r(c0)
             if i >= 2:
                 exit_y(i - 2)
+            if i == last:
+                round_y(last)
             finish(i)
-            if chunks:
-                quant_r(c1)
             if i >= 2:
                 quant_y(i - 2)
-            if c1 + 2 < CHUNKS:
-                widen(c0 + 2)
-                widen(c1 + 2)
-        exit_y(UNITS - 2)
-        round_y(UNITS - 1)
-        quant_y(UNITS - 2)
-        exit_y(UNITS - 1)
-        quant_y(UNITS - 1)
+        exit_y(last - 1)
+        quant_y(last - 1)
+        exit_y(last)
+        quant_y(last)

@@ -24,22 +24,30 @@ PASSES = K // K_PASS
 DAY_TILES = T // P
 N_TILE = 512
 HALVES = N // N_TILE
-CHUNK = 2 * K_PASS
-CHUNKS = DAY_TILES * K // CHUNK
+CHUNK_PASSES = 2
+CHUNK = CHUNK_PASSES * K_PASS
+TILE_CHUNKS = K // CHUNK
+CHUNKS = DAY_TILES * TILE_CHUNKS
 BLOCKS = CHUNK // KB
 UNITS = DAY_TILES * HALVES
+QUADRANTS = 4
+
 EARLY_TILES = 2
-EXIT_LAG = 2
-FIRST_MULTIPLY = 10
-AHEAD = 3
+VECTOR_BLOCKS = 12
+FIRST_MULTIPLY = 11
+SUM_BANKS = 4
+TURN_BANKS = 4
+SCALAR_TAIL = 3
+BACKLOG = 5
 
 
 def tile_factor_return_symlog_b13_kernel(tc, R_bytes, R_scale, B, inv_vol, gain, out_0, out_1, out_2):
     nc = tc.nc
+    last = UNITS - 1
     with ExitStack() as ctx:
         keep = ctx.enter_context(tc.tile_pool(name="keep", bufs=1))
         work = ctx.enter_context(tc.tile_pool(name="work", bufs=3))
-        psum = ctx.enter_context(tc.psum_pool(name="psum", bufs=2))
+        psum = ctx.enter_context(tc.psum_pool(name="psum", bufs=TURN_BANKS))
         ctx.enter_context(tc.manual_schedule())
 
         ident = keep.tile([P, P], F32, name="ident")
@@ -55,103 +63,90 @@ def tile_factor_return_symlog_b13_kernel(tc, R_bytes, R_scale, B, inv_vol, gain,
         rs_early = keep.tile([P, EARLY_TILES, K // KB], F32, name="rs_early")
         rs_late = keep.tile([P, DAY_TILES - EARLY_TILES, K // KB], F32, name="rs_late")
         r_raw = [keep.tile([P, K], U8, name="r_raw%d" % t) for t in range(DAY_TILES)]
+        pieces = [(g, h) for h in range(HALVES) for g in range(PASSES)]
         b_raw = {}
-        for h in range(HALVES):
-            for g in range(PASSES):
-                b_raw[(g, h)] = keep.tile([P, PACK, N_TILE], BF16, name="b_raw%d_%d" % (g, h))
+        for g, h in pieces:
+            b_raw[(g, h)] = keep.tile([P, PACK, N_TILE], BF16, name="b_raw%d_%d" % (g, h))
         gain_bc = keep.tile([P, N], BF16, name="gain_bc")
 
-        def load_r(t):
+        nc.sync.dma_start(out=rs_early[:], in_=scale_view[:, :EARLY_TILES, :])
+        for t in range(DAY_TILES):
+            if t == EARLY_TILES:
+                nc.sync.dma_start(out=rs_late[:], in_=scale_view[:, EARLY_TILES:, :])
+            if t == PASSES:
+                nc.sync.dma_start(out=iv_rows[:DAY_TILES, :], in_=inv_vol.rearrange("(t p) o -> t (p o)", p=P))
+                nc.sync.dma_start(out=gain_bc[:], in_=gain.rearrange("o n -> (o n)").partition_broadcast(P))
             nc.sync.dma_start(out=r_raw[t][:], in_=R_bytes[t * P : (t + 1) * P, :])
-
-        def load_b(g, h):
+            g, h = pieces[t]
             rows = B[g * K_PASS : (g + 1) * K_PASS, h * N_TILE : (h + 1) * N_TILE]
             nc.sync.dma_start(out=b_raw[(g, h)][:], in_=rows.rearrange("(p j) n -> p j n", j=PACK))
 
-        nc.sync.dma_start(out=rs_early[:], in_=scale_view[:, :EARLY_TILES, :])
-        load_r(0)
-        load_b(0, 0)
-        load_r(1)
-        load_b(1, 0)
-        nc.sync.dma_start(out=rs_late[:], in_=scale_view[:, EARLY_TILES:, :])
-        load_r(2)
-        load_b(2, 0)
-        load_r(3)
-        load_b(3, 0)
-        nc.sync.dma_start(out=iv_rows[:DAY_TILES, :], in_=inv_vol.rearrange("(t p) o -> t (p o)", p=P))
-        nc.sync.dma_start(out=gain_bc[:], in_=gain.rearrange("o n -> (o n)").partition_broadcast(P))
-        for g in range(PASSES):
-            load_r(4 + g)
-            load_b(g, 1)
-
         r_wide, r_bank, r_grouped, r_codes, r_scales = {}, {}, {}, {}, {}
         b_grouped, b_codes, b_scales = {}, {}, {}
-        z, mag, sgn, lg, sg, y, y_half, y_bank, y_grouped = {}, {}, {}, {}, {}, {}, {}, {}, {}
+        z, sgn, lg, sg, y, y_bank, y_grouped = {}, {}, {}, {}, {}, {}, {}
         iv = keep.tile([P, DAY_TILES], F32, name="iv")
         y_scales = keep.tile([P, HALVES, T], U8, name="y_scales", align_bytes=64)
 
-        def scale_cols(c):
-            t, half = divmod(c, 2)
-            tile = rs_early[:, t, :] if t < EARLY_TILES else rs_late[:, t - EARLY_TILES, :]
-            return tile[:, half * BLOCKS : (half + 1) * BLOCKS]
-
-        def widen(c, on_vector):
-            t, half = divmod(c, 2)
-            src = r_raw[t][:, half * CHUNK : (half + 1) * CHUNK].bitcast(FP8)
+        def widen(c):
+            t, part = divmod(c, TILE_CHUNKS)
+            src = r_raw[t][:, part * CHUNK : (part + 1) * CHUNK].bitcast(FP8)
+            scales = rs_early[:, t, :] if t < EARLY_TILES else rs_late[:, t - EARLY_TILES, :]
             r_wide[c] = work.tile([P, CHUNK], BF16, name="r_wide", bufs=6)
-            cols = scale_cols(c)
             for b in range(BLOCKS):
                 span = slice(b * KB, (b + 1) * KB)
-                if b < BLOCKS - on_vector:
-                    nc.scalar.activation(out=r_wide[c][:, span], in_=src[:, span], func=ACT.Copy, scale=cols[:, b : b + 1])
+                scale = scales[:, part * BLOCKS + b : part * BLOCKS + b + 1]
+                if b < BLOCKS - VECTOR_BLOCKS:
+                    nc.scalar.activation(out=r_wide[c][:, span], in_=src[:, span], func=ACT.Copy, scale=scale)
                 else:
-                    nc.vector.tensor_scalar(out=r_wide[c][:, span], in0=src[:, span], scalar1=cols[:, b : b + 1], scalar2=None, op0=ALU.mult)
+                    nc.vector.tensor_scalar(out=r_wide[c][:, span], in0=src[:, span], scalar1=scale, scalar2=None, op0=ALU.mult)
 
         def turn_r(c):
             words = r_wide[c][:].bitcast(F32)
-            r_bank[c] = psum.tile([P, 4, P], F32, name="r_bank", bufs=2)
-            for gl in range(2):
+            r_bank[c] = psum.tile([P, 2 * CHUNK_PASSES, P], F32, name="turn_bank")
+            for gl in range(CHUNK_PASSES):
                 for u in range(2):
-                    nc.tensor.transpose(r_bank[c][:, 2 * gl + u, :], words[:, 256 * gl + u : 256 * (gl + 1) : 2], ident[:])
+                    every_second = words[:, 2 * P * gl + u : 2 * P * (gl + 1) : 2]
+                    nc.tensor.transpose(r_bank[c][:, 2 * gl + u, :], every_second, ident[:])
 
         def exit_r(c):
             r_grouped[c] = work.tile([P, CHUNK], BF16, name="r_grouped", align_bytes=64)
-            nc.vector.tensor_copy(
-                out=r_grouped[c][:].bitcast(F32).rearrange("p (g r u) -> p g r u", g=2, u=2),
-                in_=r_bank[c][:].rearrange("p (g u) r -> p g r u", u=2),
+            copy = nc.scalar.copy if c < CHUNKS - TILE_CHUNKS else nc.vector.tensor_copy
+            copy(
+                out=r_grouped[c][:].bitcast(F32).rearrange("p (g d u) -> p g d u", g=CHUNK_PASSES, u=2),
+                in_=r_bank[c][:].rearrange("p (g u) d -> p g d u", u=2),
             )
 
         def quant_r(c):
-            r_codes[c] = keep.tile([P, 2 * P], U32, name="r_codes%d" % c, align_bytes=64)
-            r_scales[c] = keep.tile([P, 2 * P], U8, name="r_scales%d" % c, align_bytes=64)
+            r_codes[c] = keep.tile([P, CHUNK_PASSES * P], U32, name="r_codes%d" % c, align_bytes=64)
+            r_scales[c] = keep.tile([P, CHUNK_PASSES * P], U8, name="r_scales%d" % c, align_bytes=64)
             nc.vector.quantize_mx(out=r_codes[c][:].bitcast(E5X4), scales=r_scales[c][:], in_=r_grouped[c][:])
 
-        def weave_b(g, h):
-            b_grouped[(g, h)] = work.tile([P, N_TILE, PACK], BF16, name="b_grouped", align_bytes=64)
+        def weave_b(piece):
+            b_grouped[piece] = work.tile([P, N_TILE, PACK], BF16, name="b_grouped", align_bytes=64)
             nc.vector.tensor_copy(
-                out=b_grouped[(g, h)][:].rearrange("p (c i) t -> p c t i", i=4),
-                in_=b_raw[(g, h)][:].rearrange("p t (c i) -> p c t i", i=4),
+                out=b_grouped[piece][:].rearrange("p (c i) t -> p c t i", i=4),
+                in_=b_raw[piece][:].rearrange("p t (c i) -> p c t i", i=4),
             )
 
-        def quant_b(g, h):
-            b_codes[(g, h)] = keep.tile([P, N_TILE], U32, name="b_codes%d_%d" % (g, h), align_bytes=64)
-            b_scales[(g, h)] = keep.tile([P, N_TILE], U8, name="b_scales%d_%d" % (g, h), align_bytes=64)
+        def quant_b(piece):
+            b_codes[piece] = keep.tile([P, N_TILE], U32, name="b_codes%d_%d" % piece, align_bytes=64)
+            b_scales[piece] = keep.tile([P, N_TILE], U8, name="b_scales%d_%d" % piece, align_bytes=64)
             nc.vector.quantize_mx(
-                out=b_codes[(g, h)][:].bitcast(E4X4),
-                scales=b_scales[(g, h)][:],
-                in_=b_grouped[(g, h)][:].rearrange("p n t -> p (n t)"),
+                out=b_codes[piece][:].bitcast(E4X4),
+                scales=b_scales[piece][:],
+                in_=b_grouped[piece][:].rearrange("p n t -> p (n t)"),
             )
 
         def multiply(i):
             h, t = divmod(i, DAY_TILES)
-            z[i] = psum.tile([P, N_TILE], F32, name="z", bufs=4)
+            z[i] = psum.tile([P, N_TILE], F32, name="z", bufs=SUM_BANKS)
             for g in range(PASSES):
-                c, gl = 2 * t + g // 2, g % 2
-                cols = slice(gl * P, (gl + 1) * P)
+                c, gl = TILE_CHUNKS * t + g // CHUNK_PASSES, g % CHUNK_PASSES
+                days = slice(gl * P, (gl + 1) * P)
                 nc.tensor.matmul_mx(
                     out=z[i][:],
-                    lhsT=r_codes[c][:, cols].bitcast(E5X4),
-                    lhsT_scale=r_scales[c][:, cols],
+                    lhsT=r_codes[c][:, days].bitcast(E5X4),
+                    lhsT_scale=r_scales[c][:, days],
                     rhs=b_codes[(g, h)][:].bitcast(E4X4),
                     rhs_scale=b_scales[(g, h)][:],
                     start=(g == 0),
@@ -160,12 +155,12 @@ def tile_factor_return_symlog_b13_kernel(tc, R_bytes, R_scale, B, inv_vol, gain,
 
         def compress(i):
             t = i % DAY_TILES
-            mag[i] = work.tile([P, N_TILE], F32, name="mag", bufs=2)
-            sgn[i] = work.tile([P, N_TILE], BF16, name="sgn", bufs=5)
-            lg[i] = work.tile([P, N_TILE], F32, name="lg", bufs=5)
-            nc.scalar.activation(out=mag[i][:], in_=z[i][:], func=ACT.Abs, scale=iv[:, t : t + 1])
+            mag = work.tile([P, N_TILE], F32, name="mag", bufs=2)
+            sgn[i] = work.tile([P, N_TILE], BF16, name="sgn", bufs=BACKLOG)
+            lg[i] = work.tile([P, N_TILE], F32, name="lg", bufs=BACKLOG)
+            nc.scalar.activation(out=mag[:], in_=z[i][:], func=ACT.Abs, scale=iv[:, t : t + 1])
             nc.scalar.activation(out=sgn[i][:], in_=z[i][:], func=ACT.Sign, scale=iv[:, t : t + 1])
-            nc.scalar.activation(out=lg[i][:], in_=mag[i][:], func=ACT.Ln, bias=1.0)
+            nc.scalar.activation(out=lg[i][:], in_=mag[:], func=ACT.Ln, bias=1.0)
 
         def signed_gain(i):
             h = i // DAY_TILES
@@ -178,27 +173,27 @@ def tile_factor_return_symlog_b13_kernel(tc, R_bytes, R_scale, B, inv_vol, gain,
             nc.vector.tensor_tensor(out=y[i][:], in0=lg[i][:], in1=sg[i][:], op=ALU.mult)
             nc.sync.dma_start(out=out_0[t * P : (t + 1) * P, h * N_TILE : (h + 1) * N_TILE], in_=y[i][:])
 
-        def by_half(tile):
+        def by_pair(tile):
             return tile[:].rearrange("p (q u e) -> p u q e", u=2, e=2)
 
         def round_y(i):
-            y_half[i] = work.tile([P, N_TILE], BF16, name="y_half")
-            sorted_out = y_half[i][:].rearrange("p (u q e) -> p u q e", u=2, e=2)
-            if i == UNITS - 1:
-                nc.vector.tensor_tensor(out=sorted_out, in0=by_half(lg[i]), in1=by_half(sg[i]), op=ALU.mult)
+            y_half = work.tile([P, N_TILE], BF16, name="y_half")
+            sorted_out = y_half[:].rearrange("p (u q e) -> p u q e", u=2, e=2)
+            if i == last:
+                nc.vector.tensor_tensor(out=sorted_out, in0=by_pair(lg[i]), in1=by_pair(sg[i]), op=ALU.mult)
             else:
-                nc.vector.tensor_copy(out=sorted_out, in_=by_half(y[i]))
-            words = y_half[i][:].bitcast(F32)
-            y_bank[i] = psum.tile([P, 2, P], F32, name="y_bank", bufs=2)
+                nc.vector.tensor_copy(out=sorted_out, in_=by_pair(y[i]))
+            words = y_half[:].bitcast(F32)
+            y_bank[i] = psum.tile([P, 2, P], F32, name="turn_bank")
             for u in range(2):
                 nc.tensor.transpose(y_bank[i][:, u, :], words[:, u * P : (u + 1) * P], ident[:])
 
         def exit_y(i):
             y_grouped[i] = work.tile([P, N_TILE], BF16, name="y_grouped", align_bytes=64)
-            copy = nc.scalar.copy if i >= UNITS - 3 else nc.vector.tensor_copy
+            copy = nc.scalar.copy if i >= UNITS - SCALAR_TAIL else nc.vector.tensor_copy
             copy(
-                out=y_grouped[i][:].bitcast(F32).rearrange("p (r u) -> p r u", u=2),
-                in_=y_bank[i][:].rearrange("p u r -> p r u"),
+                out=y_grouped[i][:].bitcast(F32).rearrange("p (d u) -> p d u", u=2),
+                in_=y_bank[i][:].rearrange("p u d -> p d u"),
             )
 
         def quant_y(i):
@@ -209,44 +204,14 @@ def tile_factor_return_symlog_b13_kernel(tc, R_bytes, R_scale, B, inv_vol, gain,
             words_out = out_1[h].rearrange("p m t -> p (m t)").bitcast(I32)
             nc.sync.dma_start(out=words_out[:, days], in_=codes[:].bitcast(I32))
             if t == DAY_TILES - 1:
-                for q in range(4):
-                    queue = nc.sync if q % 2 == 0 or h == 0 else nc.scalar
+                for q in range(QUADRANTS):
+                    queue = nc.scalar if i == last and q % 2 == 1 else nc.sync
                     queue.dma_start(
                         out=out_2[h, 4 * q : 4 * q + 4, :].bitcast(I32),
                         in_=y_scales[32 * q : 32 * q + 4, h, :].bitcast(I32),
                     )
 
-        pieces = [(g, h) for h in range(HALVES) for g in range(PASSES)]
-        iv_wide = keep.tile([P, P], F32, name="iv_wide")
-        issued = 0
-        for c in range(CHUNKS + EXIT_LAG + 1):
-            if c < CHUNKS:
-                widen(c, {1: BLOCKS, CHUNKS - 1: BLOCKS // 2}.get(c, 0))
-            if c % 2 == 1 and c // 2 < len(pieces):
-                weave_b(*pieces[c // 2])
-            if 0 <= c - EXIT_LAG < CHUNKS:
-                turn_r(c - EXIT_LAG)
-            if c == FIRST_MULTIPLY - 1:
-                nc.vector.tensor_copy(out=iv_wide[:], in_=iv_rows[:])
-                iv_bank = psum.tile([P, 2, P], F32, name="y_bank", bufs=2)
-                nc.tensor.transpose(iv_bank[:, 0, :], iv_wide[:], ident[:])
-            if c >= FIRST_MULTIPLY and issued <= AHEAD:
-                multiply(issued)
-                issued = issued + 1
-            if 0 <= c - EXIT_LAG < CHUNKS:
-                exit_r(c - EXIT_LAG)
-            if c == FIRST_MULTIPLY:
-                nc.vector.tensor_copy(out=iv[:], in_=iv_bank[:, 0, :DAY_TILES])
-            if c % 2 == 0 and 0 <= c // 2 - 1 < len(pieces):
-                quant_b(*pieces[c // 2 - 1])
-            if 0 <= c - EXIT_LAG - 1 < CHUNKS:
-                quant_r(c - EXIT_LAG - 1)
-        last = UNITS - 1
-        for i in range(UNITS):
-            if issued <= min(i + AHEAD, last):
-                multiply(issued)
-                issued = issued + 1
-            compress(i)
+        def vector_step(i):
             signed_gain(i)
             if i >= 1:
                 round_y(i - 1)
@@ -257,7 +222,40 @@ def tile_factor_return_symlog_b13_kernel(tc, R_bytes, R_scale, B, inv_vol, gain,
             finish(i)
             if i >= 2:
                 quant_y(i - 2)
-        exit_y(last - 1)
-        quant_y(last - 1)
-        exit_y(last)
-        quant_y(last)
+
+        issued = 0
+        for c in range(CHUNKS + 3):
+            if c < CHUNKS:
+                widen(c)
+            if c == FIRST_MULTIPLY - 1:
+                iv_wide = keep.tile([P, P], F32, name="iv_wide")
+                nc.vector.tensor_copy(out=iv_wide[:], in_=iv_rows[:])
+                iv_bank = psum.tile([P, P], F32, name="turn_bank")
+                nc.tensor.transpose(iv_bank[:], iv_wide[:], ident[:])
+            if c >= FIRST_MULTIPLY and issued < SUM_BANKS:
+                multiply(issued)
+                issued = issued + 1
+            if 0 <= c - 1 < CHUNKS:
+                turn_r(c - 1)
+            if c % 2 == 1 and c // 2 < len(pieces):
+                weave_b(pieces[c // 2])
+            if 0 <= c - 2 < CHUNKS:
+                exit_r(c - 2)
+            if c == FIRST_MULTIPLY:
+                nc.vector.tensor_copy(out=iv[:], in_=iv_bank[:, :DAY_TILES])
+            if c % 2 == 0 and 0 <= c // 2 - 1 < len(pieces):
+                quant_b(pieces[c // 2 - 1])
+            if 0 <= c - 3 < CHUNKS:
+                quant_r(c - 3)
+
+        for i in range(UNITS):
+            if i >= 1 and issued <= last:
+                multiply(issued)
+                issued = issued + 1
+            compress(i)
+            if i >= 1:
+                vector_step(i - 1)
+        vector_step(last)
+        for i in (last - 1, last):
+            exit_y(i)
+            quant_y(i)

from contextlib import ExitStack

import concourse.mybir as mybir
from concourse.masks import make_identity

T, K, N, KB = 1024, 2048, 1024, 32
FLOPS = 2 * T * K * N

F32 = mybir.dt.float32
BF16 = mybir.dt.bfloat16
U32 = mybir.dt.uint32
I32 = mybir.dt.int32
U8 = mybir.dt.uint8
FP8 = mybir.dt.float8_e4m3fn
E4X4 = mybir.dt.float8_e4m3fn_x4
E5X4 = mybir.dt.float8_e5m2_x4
ACT = mybir.ActivationFunctionType
ALU = mybir.AluOpType

P = 128
PACK = 4
K_PASS = P * PACK
PASSES = K // K_PASS
DAY_TILES = T // P
N_TILE = 512
HALVES = N // N_TILE
CHUNK_PASSES = 2
CHUNK = CHUNK_PASSES * K_PASS
TILE_CHUNKS = K // CHUNK
CHUNKS = DAY_TILES * TILE_CHUNKS
BLOCKS = CHUNK // KB
UNITS = DAY_TILES * HALVES
QUADRANTS = 4

EARLY_TILES = 2
VECTOR_BLOCKS = 12
FIRST_MULTIPLY = 11
SUM_BANKS = 4
TURN_BANKS = 4
SCALAR_TAIL = 3
BACKLOG = 5


def tile_factor_return_symlog_b13_kernel(tc, R_bytes, R_scale, B, inv_vol, gain, out_0, out_1, out_2):
    nc = tc.nc
    last = UNITS - 1
    with ExitStack() as ctx:
        keep = ctx.enter_context(tc.tile_pool(name="keep", bufs=1))
        work = ctx.enter_context(tc.tile_pool(name="work", bufs=3))
        psum = ctx.enter_context(tc.psum_pool(name="psum", bufs=TURN_BANKS))
        ctx.enter_context(tc.manual_schedule())

        ident = keep.tile([P, P], F32, name="ident")
        iv_rows = keep.tile([P, P], BF16, name="iv_rows")
        warm = keep.tile([P, 1], F32, name="warm")
        warm_out = keep.tile([P, 1], F32, name="warm_out")
        nc.vector.memset(warm[:], 1.0)
        nc.scalar.activation(out=warm_out[:], in_=warm[:], func=ACT.Ln)
        nc.gpsimd.memset(iv_rows[:], 0.0)
        make_identity(nc, ident[:])

        scale_view = R_scale.rearrange("(t p) b -> p t b", p=P)
        rs_early = keep.tile([P, EARLY_TILES, K // KB], F32, name="rs_early")
        rs_late = keep.tile([P, DAY_TILES - EARLY_TILES, K // KB], F32, name="rs_late")
        r_raw = [keep.tile([P, K], U8, name="r_raw%d" % t) for t in range(DAY_TILES)]
        pieces = [(g, h) for h in range(HALVES) for g in range(PASSES)]
        b_raw = {}
        for g, h in pieces:
            b_raw[(g, h)] = keep.tile([P, PACK, N_TILE], BF16, name="b_raw%d_%d" % (g, h))
        gain_bc = keep.tile([P, N], BF16, name="gain_bc")

        nc.sync.dma_start(out=rs_early[:], in_=scale_view[:, :EARLY_TILES, :])
        for t in range(DAY_TILES):
            if t == EARLY_TILES:
                nc.sync.dma_start(out=rs_late[:], in_=scale_view[:, EARLY_TILES:, :])
            if t == PASSES:
                nc.sync.dma_start(out=iv_rows[:DAY_TILES, :], in_=inv_vol.rearrange("(t p) o -> t (p o)", p=P))
                nc.sync.dma_start(out=gain_bc[:], in_=gain.rearrange("o n -> (o n)").partition_broadcast(P))
            nc.sync.dma_start(out=r_raw[t][:], in_=R_bytes[t * P : (t + 1) * P, :])
            g, h = pieces[t]
            rows = B[g * K_PASS : (g + 1) * K_PASS, h * N_TILE : (h + 1) * N_TILE]
            nc.sync.dma_start(out=b_raw[(g, h)][:], in_=rows.rearrange("(p j) n -> p j n", j=PACK))

        r_wide, r_bank, r_grouped, r_codes, r_scales = {}, {}, {}, {}, {}
        b_grouped, b_codes, b_scales = {}, {}, {}
        z, sgn, lg, sg, y, y_bank, y_grouped = {}, {}, {}, {}, {}, {}, {}
        iv = keep.tile([P, DAY_TILES], F32, name="iv")
        y_scales = keep.tile([P, HALVES, T], U8, name="y_scales", align_bytes=64)

        def widen(c):
            t, part = divmod(c, TILE_CHUNKS)
            src = r_raw[t][:, part * CHUNK : (part + 1) * CHUNK].bitcast(FP8)
            scales = rs_early[:, t, :] if t < EARLY_TILES else rs_late[:, t - EARLY_TILES, :]
            r_wide[c] = work.tile([P, CHUNK], BF16, name="r_wide", bufs=6)
            for b in range(BLOCKS):
                span = slice(b * KB, (b + 1) * KB)
                scale = scales[:, part * BLOCKS + b : part * BLOCKS + b + 1]
                if b < BLOCKS - VECTOR_BLOCKS:
                    nc.scalar.activation(out=r_wide[c][:, span], in_=src[:, span], func=ACT.Copy, scale=scale)
                else:
                    nc.vector.tensor_scalar(out=r_wide[c][:, span], in0=src[:, span], scalar1=scale, scalar2=None, op0=ALU.mult)

        def turn_r(c):
            words = r_wide[c][:].bitcast(F32)
            r_bank[c] = psum.tile([P, 2 * CHUNK_PASSES, P], F32, name="turn_bank")
            for gl in range(CHUNK_PASSES):
                for u in range(2):
                    every_second = words[:, 2 * P * gl + u : 2 * P * (gl + 1) : 2]
                    nc.tensor.transpose(r_bank[c][:, 2 * gl + u, :], every_second, ident[:])

        def exit_r(c):
            r_grouped[c] = work.tile([P, CHUNK], BF16, name="r_grouped", align_bytes=64)
            copy = nc.scalar.copy if c < CHUNKS - TILE_CHUNKS else nc.vector.tensor_copy
            copy(
                out=r_grouped[c][:].bitcast(F32).rearrange("p (g d u) -> p g d u", g=CHUNK_PASSES, u=2),
                in_=r_bank[c][:].rearrange("p (g u) d -> p g d u", u=2),
            )

        def quant_r(c):
            r_codes[c] = keep.tile([P, CHUNK_PASSES * P], U32, name="r_codes%d" % c, align_bytes=64)
            r_scales[c] = keep.tile([P, CHUNK_PASSES * P], U8, name="r_scales%d" % c, align_bytes=64)
            nc.vector.quantize_mx(out=r_codes[c][:].bitcast(E5X4), scales=r_scales[c][:], in_=r_grouped[c][:])

        def weave_b(piece):
            b_grouped[piece] = work.tile([P, N_TILE, PACK], BF16, name="b_grouped", align_bytes=64)
            nc.vector.tensor_copy(
                out=b_grouped[piece][:].rearrange("p (c i) t -> p c t i", i=4),
                in_=b_raw[piece][:].rearrange("p t (c i) -> p c t i", i=4),
            )

        def quant_b(piece):
            b_codes[piece] = keep.tile([P, N_TILE], U32, name="b_codes%d_%d" % piece, align_bytes=64)
            b_scales[piece] = keep.tile([P, N_TILE], U8, name="b_scales%d_%d" % piece, align_bytes=64)
            nc.vector.quantize_mx(
                out=b_codes[piece][:].bitcast(E4X4),
                scales=b_scales[piece][:],
                in_=b_grouped[piece][:].rearrange("p n t -> p (n t)"),
            )

        def multiply(i):
            h, t = divmod(i, DAY_TILES)
            z[i] = psum.tile([P, N_TILE], F32, name="z", bufs=SUM_BANKS)
            for g in range(PASSES):
                c, gl = TILE_CHUNKS * t + g // CHUNK_PASSES, g % CHUNK_PASSES
                days = slice(gl * P, (gl + 1) * P)
                nc.tensor.matmul_mx(
                    out=z[i][:],
                    lhsT=r_codes[c][:, days].bitcast(E5X4),
                    lhsT_scale=r_scales[c][:, days],
                    rhs=b_codes[(g, h)][:].bitcast(E4X4),
                    rhs_scale=b_scales[(g, h)][:],
                    start=(g == 0),
                    stop=(g == PASSES - 1),
                )

        def compress(i):
            t = i % DAY_TILES
            mag = work.tile([P, N_TILE], F32, name="mag", bufs=2)
            sgn[i] = work.tile([P, N_TILE], BF16, name="sgn", bufs=BACKLOG)
            lg[i] = work.tile([P, N_TILE], F32, name="lg", bufs=BACKLOG)
            nc.scalar.activation(out=mag[:], in_=z[i][:], func=ACT.Abs, scale=iv[:, t : t + 1])
            nc.scalar.activation(out=sgn[i][:], in_=z[i][:], func=ACT.Sign, scale=iv[:, t : t + 1])
            nc.scalar.activation(out=lg[i][:], in_=mag[:], func=ACT.Ln, bias=1.0)

        def signed_gain(i):
            h = i // DAY_TILES
            sg[i] = work.tile([P, N_TILE], BF16, name="sg", bufs=2)
            nc.vector.tensor_tensor(out=sg[i][:], in0=sgn[i][:], in1=gain_bc[:, h * N_TILE : (h + 1) * N_TILE], op=ALU.mult)

        def finish(i):
            h, t = divmod(i, DAY_TILES)
            y[i] = work.tile([P, N_TILE], F32, name="y", bufs=4)
            nc.vector.tensor_tensor(out=y[i][:], in0=lg[i][:], in1=sg[i][:], op=ALU.mult)
            nc.sync.dma_start(out=out_0[t * P : (t + 1) * P, h * N_TILE : (h + 1) * N_TILE], in_=y[i][:])

        def by_pair(tile):
            return tile[:].rearrange("p (q u e) -> p u q e", u=2, e=2)

        def round_y(i):
            y_half = work.tile([P, N_TILE], BF16, name="y_half")
            sorted_out = y_half[:].rearrange("p (u q e) -> p u q e", u=2, e=2)
            if i == last:
                nc.vector.tensor_tensor(out=sorted_out, in0=by_pair(lg[i]), in1=by_pair(sg[i]), op=ALU.mult)
            else:
                nc.vector.tensor_copy(out=sorted_out, in_=by_pair(y[i]))
            words = y_half[:].bitcast(F32)
            y_bank[i] = psum.tile([P, 2, P], F32, name="turn_bank")
            for u in range(2):
                nc.tensor.transpose(y_bank[i][:, u, :], words[:, u * P : (u + 1) * P], ident[:])

        def exit_y(i):
            y_grouped[i] = work.tile([P, N_TILE], BF16, name="y_grouped", align_bytes=64)
            copy = nc.scalar.copy if i >= UNITS - SCALAR_TAIL else nc.vector.tensor_copy
            copy(
                out=y_grouped[i][:].bitcast(F32).rearrange("p (d u) -> p d u", u=2),
                in_=y_bank[i][:].rearrange("p u d -> p d u"),
            )

        def quant_y(i):
            h, t = divmod(i, DAY_TILES)
            days = slice(t * P, (t + 1) * P)
            codes = work.tile([P, P], U32, name="y_codes", bufs=4, align_bytes=64)
            nc.vector.quantize_mx(out=codes[:].bitcast(E4X4), scales=y_scales[:, h, days], in_=y_grouped[i][:])
            words_out = out_1[h].rearrange("p m t -> p (m t)").bitcast(I32)
            nc.sync.dma_start(out=words_out[:, days], in_=codes[:].bitcast(I32))
            if t == DAY_TILES - 1:
                for q in range(QUADRANTS):
                    queue = nc.scalar if i == last and q % 2 == 1 else nc.sync
                    queue.dma_start(
                        out=out_2[h, 4 * q : 4 * q + 4, :].bitcast(I32),
                        in_=y_scales[32 * q : 32 * q + 4, h, :].bitcast(I32),
                    )

        def vector_step(i):
            signed_gain(i)
            if i >= 1:
                round_y(i - 1)
            if i >= 2:
                exit_y(i - 2)
            if i == last:
                round_y(last)
            finish(i)
            if i >= 2:
                quant_y(i - 2)

        issued = 0
        for c in range(CHUNKS + 3):
            if c < CHUNKS:
                widen(c)
            if c == FIRST_MULTIPLY - 1:
                iv_wide = keep.tile([P, P], F32, name="iv_wide")
                nc.vector.tensor_copy(out=iv_wide[:], in_=iv_rows[:])
                iv_bank = psum.tile([P, P], F32, name="turn_bank")
                nc.tensor.transpose(iv_bank[:], iv_wide[:], ident[:])
            if c >= FIRST_MULTIPLY and issued < SUM_BANKS:
                multiply(issued)
                issued = issued + 1
            if 0 <= c - 1 < CHUNKS:
                turn_r(c - 1)
            if c % 2 == 1 and c // 2 < len(pieces):
                weave_b(pieces[c // 2])
            if 0 <= c - 2 < CHUNKS:
                exit_r(c - 2)
            if c == FIRST_MULTIPLY:
                nc.vector.tensor_copy(out=iv[:], in_=iv_bank[:, :DAY_TILES])
            if c % 2 == 0 and 0 <= c // 2 - 1 < len(pieces):
                quant_b(pieces[c // 2 - 1])
            if 0 <= c - 3 < CHUNKS:
                quant_r(c - 3)

        for i in range(UNITS):
            if i >= 1 and issued <= last:
                multiply(issued)
                issued = issued + 1
            compress(i)
            if i >= 1:
                vector_step(i - 1)
        vector_step(last)
        for i in (last - 1, last):
            exit_y(i)
            quant_y(i)
